import numpy as np
CORES = [64,68,72,76,80,84,88,92,96,100,104,108,112,116,120,124]
N = 16
def setup_inputs(rng):
    return {"x1": rng.standard_normal((N, 128, 16), dtype=np.float32), "x2": rng.standard_normal((N, 128, 16), dtype=np.float32)}
def reference(x1, x2):
    out = []
    g = np.concatenate(list(x1), axis=1)
    out.append(np.broadcast_to(g, (N,) + g.shape))
    s = x2.sum(axis=0, dtype=np.float64).astype(x2.dtype)
    out.append(np.broadcast_to(s, (N,) + s.shape))
    return {"y1": out[0], "y2": out[1]}

@@ -1,0 +1,77 @@
+from concourse.bass import DstId, RemoteDMATransfer
+from concourse.mybir import AluOpType
+
+W = 16
+
+SCRATCH = {
+    "stage": ("sbuf", [128, 2 * W], "float32"),
+    "pair": ("sbuf", [128, 2 * W], "float32"),
+    "xs": ("sbuf", [128, 8 * W], "float32"),
+    "gath": ("sbuf", [128, 16 * W], "float32"),
+    "part": ("sbuf", [128, 2 * W], "float32"),
+}
+SEMAPHORES = ["loaded", "sent", "in1", "in2", "got1", "got2", "added", "st1", "st2"]
+
+HELPERS = (2, 6, 3, 7)
+SUMMER = 2
+OFF_CHIP = 0x00FF
+
+
+def rank_program(g, core, T, topo):
+    chips = sorted(set(topo.chip(c) for c in T.cores))
+    chip, k = topo.chip(core), core % 8
+    if chip not in chips:
+        return
+    base = chips[0]
+    p = chip & 1
+    plane = [c for c in chips if (c & 1) == p]
+
+    def dst(c):
+        rid, pid, _se = topo.addr(c)
+        return DstId(rid=rid, pnc=pid)
+
+    rank = T.rank_of(core)
+    if rank is not None:
+        m, e = (chip - base) // 2, k // 4
+        g.sync.dma_start(T.stage[:, 0:W], T.x1[:]).then_inc(T.sem.loaded, 16)
+        g.scalar.dma_start(T.stage[:, W:2 * W], T.x2[:]).then_inc(T.sem.loaded, 16)
+        g.wait_ge(T.sem.loaded, 32)
+        g.remote_dma_fused([
+            RemoteDMATransfer(dst_ids=[dst(c * 8 + HELPERS[m]) for c in plane], dma_engine_mask=0x0F,
+                              remote_sem=T.sem.in1, srcs=[T.stage[:, 0:W]],
+                              dsts=[T.pair[:, e * W:(e + 1) * W] for c in plane]),
+            RemoteDMATransfer(dst_ids=[dst(c * 8 + SUMMER) for c in plane], dma_engine_mask=0xF0,
+                              remote_sem=T.sem.in2, srcs=[T.stage[:, W:2 * W]],
+                              dsts=[T.xs[:, (2 * m + e) * W:(2 * m + e + 1) * W] for c in plane]),
+        ], local_sem=T.sem.sent)
+        g.sync.wait_ge(T.sem.got1, 8 * 8)
+        g.sync.dma_start(T.y1[:], T.gath[:]).then_inc(T.sem.st1, 16)
+        g.wait_ge(T.sem.got2, 2 * 8)
+        g.dma_start(T.part[:, 0:W], T.part[:, W:2 * W], accum_op=AluOpType.add).then_inc(T.sem.added, 16)
+        g.wait_ge(T.sem.added, 16)
+        g.dma_start(T.y2[:], T.part[:, 0:W]).then_inc(T.sem.st2, 16)
+        g.wait_ge(T.sem.st2, 16)
+        g.wait_ge(T.sem.sent, 8)
+        g.sync.wait_ge(T.sem.st1, 16)
+        return
+
+    if k not in HELPERS:
+        return
+    m = HELPERS.index(k)
+    ranks4 = [c for c in T.cores if topo.chip(c) in (chip, chip ^ 1)]
+    col = (4 * m + 2 * p) * W
+    g.wait_ge(T.sem.in1, 2 * 4)
+    g.remote_dma_fused([
+        RemoteDMATransfer(dst_ids=[dst(c) for c in ranks4], dma_engine_mask=OFF_CHIP, remote_sem=T.sem.got1,
+                          srcs=[T.pair[:]], dsts=[T.gath[:, col:col + 2 * W] for c in ranks4]),
+    ], local_sem=T.sem.sent)
+    sent = 8
+    if k == SUMMER:
+        g.wait_ge(T.sem.in2, 8 * 4)
+        g.remote_dma_fused([
+            RemoteDMATransfer(dst_ids=[dst(c) for c in ranks4], dma_engine_mask=OFF_CHIP, remote_sem=T.sem.got2,
+                              srcs=[T.xs[:, i * W:(i + 1) * W] for i in range(8)],
+                              dsts=[T.part[:, p * W:(p + 1) * W] for c in ranks4], alu_op=1),
+        ], local_sem=T.sem.sent)
+        sent += 8
+    g.wait_ge(T.sem.sent, sent)

@@ -4,17 +4,17 @@ from concourse.mybir import AluOpType
 W = 16
 
 SCRATCH = {
-    "stage": ("sbuf", [128, 2 * W], "float32"),
+    "st1": ("dram", [128, W], "float32"),
+    "st2": ("dram", [2, 128, W // 2], "float32"),
     "pair": ("sbuf", [128, 2 * W], "float32"),
-    "xs": ("sbuf", [128, 8 * W], "float32"),
+    "xs": ("dram", [8, 128, W // 2], "float32"),
     "gath": ("sbuf", [128, 16 * W], "float32"),
-    "part": ("sbuf", [128, 2 * W], "float32"),
+    "part": ("dram", [4, 128, W // 2], "float32"),
 }
-SEMAPHORES = ["loaded", "sent", "in1", "in2", "got1", "got2", "added", "st1", "st2"]
+SEMAPHORES = ["ld1", "ld2", "sent", "in1", "in2", "got1", "sum0", "sum1", "st1", "st2"]
 
 HELPERS = (2, 6, 3, 7)
-SUMMER = 2
-OFF_CHIP = 0x00FF
+SUMMERS = (2, 6)
 
 
 def rank_program(g, core, T, topo):
@@ -22,56 +22,67 @@ def rank_program(g, core, T, topo):
     chip, k = topo.chip(core), core % 8
     if chip not in chips:
         return
-    base = chips[0]
     p = chip & 1
-    plane = [c for c in chips if (c & 1) == p]
+    others = [c for c in chips if (c & 1) == p and c != chip]
 
     def dst(c):
         rid, pid, _se = topo.addr(c)
         return DstId(rid=rid, pnc=pid)
 
-    rank = T.rank_of(core)
-    if rank is not None:
-        m, e = (chip - base) // 2, k // 4
-        g.sync.dma_start(T.stage[:, 0:W], T.x1[:]).then_inc(T.sem.loaded, 16)
-        g.scalar.dma_start(T.stage[:, W:2 * W], T.x2[:]).then_inc(T.sem.loaded, 16)
-        g.wait_ge(T.sem.loaded, 32)
-        g.remote_dma_fused([
-            RemoteDMATransfer(dst_ids=[dst(c * 8 + HELPERS[m]) for c in plane], dma_engine_mask=0x0F,
-                              remote_sem=T.sem.in1, srcs=[T.stage[:, 0:W]],
-                              dsts=[T.pair[:, e * W:(e + 1) * W] for c in plane]),
-            RemoteDMATransfer(dst_ids=[dst(c * 8 + SUMMER) for c in plane], dma_engine_mask=0xF0,
-                              remote_sem=T.sem.in2, srcs=[T.stage[:, W:2 * W]],
-                              dsts=[T.xs[:, (2 * m + e) * W:(2 * m + e + 1) * W] for c in plane]),
-        ], local_sem=T.sem.sent)
+    def copy(cores, mask, sem, src, out):
+        return RemoteDMATransfer(dst_ids=[dst(c) for c in cores], dma_engine_mask=mask, remote_sem=sem,
+                                 srcs=[src], dsts=[out for c in cores])
+
+    if T.rank_of(core) is not None:
+        m, e = (chip - chips[0]) // 2, k // 4
+        g.scalar.dma_start(T.st2[:], T.x2[:]).then_inc(T.sem.ld2, 16)
+        g.sync.dma_start(T.st1[:], T.x1[:]).then_inc(T.sem.ld1, 16)
+        g.wait_ge(T.sem.ld2, 16)
+        slot = T.xs[2 * m + e]
+        g.remote_dma_fused(
+            [copy([c * 8 + SUMMERS[h] for c in others], 0x000F << (4 * h), T.sem.in2, T.st2[h], slot)
+             for h in range(2)] +
+            [copy([chip * 8 + SUMMERS[h]], 0x0F00 << (4 * h), T.sem.in2, T.st2[h], slot) for h in range(2)],
+            local_sem=T.sem.sent)
+        g.wait_ge(T.sem.ld1, 16)
+        half = T.pair[:, e * W:(e + 1) * W]
+        g.remote_dma_fused(
+            [copy([c * 8 + HELPERS[m] for c in others], 0x00FF, T.sem.in1, T.st1[:], half),
+             copy([chip * 8 + HELPERS[m]], 0xFF00, T.sem.in1, T.st1[:], half)],
+            local_sem=T.sem.sent)
         g.sync.wait_ge(T.sem.got1, 8 * 8)
         g.sync.dma_start(T.y1[:], T.gath[:]).then_inc(T.sem.st1, 16)
-        g.wait_ge(T.sem.got2, 2 * 8)
-        g.dma_start(T.part[:, 0:W], T.part[:, W:2 * W], accum_op=AluOpType.add).then_inc(T.sem.added, 16)
-        g.wait_ge(T.sem.added, 16)
-        g.dma_start(T.y2[:], T.part[:, 0:W]).then_inc(T.sem.st2, 16)
+        q = 1 - p
+        g.wait_ge(T.sem["sum%d" % p], 2 * 8)
+        g.dma_start(T.y2[:], T.part[2 * p:2 * p + 2]).then_inc(T.sem.st2, 16)
         g.wait_ge(T.sem.st2, 16)
-        g.wait_ge(T.sem.sent, 8)
+        g.wait_ge(T.sem["sum%d" % q], 2 * 8)
+        g.dma_start(T.y2[:], T.part[2 * q:2 * q + 2], accum_op=AluOpType.add).then_inc(T.sem.st2, 16)
+        g.wait_ge(T.sem.st2, 32)
+        g.wait_ge(T.sem.sent, 4 * 4 + 2 * 8)
         g.sync.wait_ge(T.sem.st1, 16)
         return
 
     if k not in HELPERS:
         return
-    m = HELPERS.index(k)
-    ranks4 = [c for c in T.cores if topo.chip(c) in (chip, chip ^ 1)]
-    col = (4 * m + 2 * p) * W
-    g.wait_ge(T.sem.in1, 2 * 4)
-    g.remote_dma_fused([
-        RemoteDMATransfer(dst_ids=[dst(c) for c in ranks4], dma_engine_mask=OFF_CHIP, remote_sem=T.sem.got1,
-                          srcs=[T.pair[:]], dsts=[T.gath[:, col:col + 2 * W] for c in ranks4]),
-    ], local_sem=T.sem.sent)
-    sent = 8
-    if k == SUMMER:
+    here = [c for c in T.cores if topo.chip(c) == chip]
+    mate = [c for c in T.cores if topo.chip(c) == chip ^ 1]
+    sent = 0
+    if k in SUMMERS:
+        h = SUMMERS.index(k)
         g.wait_ge(T.sem.in2, 8 * 4)
         g.remote_dma_fused([
-            RemoteDMATransfer(dst_ids=[dst(c) for c in ranks4], dma_engine_mask=OFF_CHIP, remote_sem=T.sem.got2,
-                              srcs=[T.xs[:, i * W:(i + 1) * W] for i in range(8)],
-                              dsts=[T.part[:, p * W:(p + 1) * W] for c in ranks4], alu_op=1),
+            RemoteDMATransfer(dst_ids=[dst(c) for c in here + mate], dma_engine_mask=0x00FF,
+                              remote_sem=T.sem["sum%d" % p], srcs=[T.xs[i] for i in range(8)],
+                              dsts=[T.part[2 * p + h] for c in here + mate], alu_op=1),
         ], local_sem=T.sem.sent)
         sent += 8
+    m = HELPERS.index(k)
+    col = (4 * m + 2 * p) * W
+    g.wait_ge(T.sem.in1, 2 * 8)
+    g.remote_dma_fused(
+        [copy(mate, 0x00FF, T.sem.got1, T.pair[:], T.gath[:, col:col + 2 * W]),
+         copy(here, 0xFF00, T.sem.got1, T.pair[:], T.gath[:, col:col + 2 * W])],
+        local_sem=T.sem.sent)
+    sent += 16
     g.wait_ge(T.sem.sent, sent)

from concourse.bass import DstId, RemoteDMATransfer
from concourse.mybir import AluOpType

W = 16

SCRATCH = {
    "st1": ("dram", [128, W], "float32"),
    "st2": ("dram", [2, 128, W // 2], "float32"),
    "pair": ("sbuf", [128, 2 * W], "float32"),
    "xs": ("dram", [8, 128, W // 2], "float32"),
    "gath": ("sbuf", [128, 16 * W], "float32"),
    "part": ("dram", [4, 128, W // 2], "float32"),
}
SEMAPHORES = ["ld1", "ld2", "sent", "in1", "in2", "got1", "sum0", "sum1", "st1", "st2"]

HELPERS = (2, 6, 3, 7)
SUMMERS = (2, 6)


def rank_program(g, core, T, topo):
    chips = sorted(set(topo.chip(c) for c in T.cores))
    chip, k = topo.chip(core), core % 8
    if chip not in chips:
        return
    p = chip & 1
    others = [c for c in chips if (c & 1) == p and c != chip]

    def dst(c):
        rid, pid, _se = topo.addr(c)
        return DstId(rid=rid, pnc=pid)

    def copy(cores, mask, sem, src, out):
        return RemoteDMATransfer(dst_ids=[dst(c) for c in cores], dma_engine_mask=mask, remote_sem=sem,
                                 srcs=[src], dsts=[out for c in cores])

    if T.rank_of(core) is not None:
        m, e = (chip - chips[0]) // 2, k // 4
        g.scalar.dma_start(T.st2[:], T.x2[:]).then_inc(T.sem.ld2, 16)
        g.sync.dma_start(T.st1[:], T.x1[:]).then_inc(T.sem.ld1, 16)
        g.wait_ge(T.sem.ld2, 16)
        slot = T.xs[2 * m + e]
        g.remote_dma_fused(
            [copy([c * 8 + SUMMERS[h] for c in others], 0x000F << (4 * h), T.sem.in2, T.st2[h], slot)
             for h in range(2)] +
            [copy([chip * 8 + SUMMERS[h]], 0x0F00 << (4 * h), T.sem.in2, T.st2[h], slot) for h in range(2)],
            local_sem=T.sem.sent)
        g.wait_ge(T.sem.ld1, 16)
        half = T.pair[:, e * W:(e + 1) * W]
        g.remote_dma_fused(
            [copy([c * 8 + HELPERS[m] for c in others], 0x00FF, T.sem.in1, T.st1[:], half),
             copy([chip * 8 + HELPERS[m]], 0xFF00, T.sem.in1, T.st1[:], half)],
            local_sem=T.sem.sent)
        g.sync.wait_ge(T.sem.got1, 8 * 8)
        g.sync.dma_start(T.y1[:], T.gath[:]).then_inc(T.sem.st1, 16)
        q = 1 - p
        g.wait_ge(T.sem["sum%d" % p], 2 * 8)
        g.dma_start(T.y2[:], T.part[2 * p:2 * p + 2]).then_inc(T.sem.st2, 16)
        g.wait_ge(T.sem.st2, 16)
        g.wait_ge(T.sem["sum%d" % q], 2 * 8)
        g.dma_start(T.y2[:], T.part[2 * q:2 * q + 2], accum_op=AluOpType.add).then_inc(T.sem.st2, 16)
        g.wait_ge(T.sem.st2, 32)
        g.wait_ge(T.sem.sent, 4 * 4 + 2 * 8)
        g.sync.wait_ge(T.sem.st1, 16)
        return

    if k not in HELPERS:
        return
    here = [c for c in T.cores if topo.chip(c) == chip]
    mate = [c for c in T.cores if topo.chip(c) == chip ^ 1]
    sent = 0
    if k in SUMMERS:
        h = SUMMERS.index(k)
        g.wait_ge(T.sem.in2, 8 * 4)
        g.remote_dma_fused([
            RemoteDMATransfer(dst_ids=[dst(c) for c in here + mate], dma_engine_mask=0x00FF,
                              remote_sem=T.sem["sum%d" % p], srcs=[T.xs[i] for i in range(8)],
                              dsts=[T.part[2 * p + h] for c in here + mate], alu_op=1),
        ], local_sem=T.sem.sent)
        sent += 8
    m = HELPERS.index(k)
    col = (4 * m + 2 * p) * W
    g.wait_ge(T.sem.in1, 2 * 8)
    g.remote_dma_fused(
        [copy(mate, 0x00FF, T.sem.got1, T.pair[:], T.gath[:, col:col + 2 * W]),
         copy(here, 0xFF00, T.sem.got1, T.pair[:], T.gath[:, col:col + 2 * W])],
        local_sem=T.sem.sent)
    sent += 16
    g.wait_ge(T.sem.sent, sent)
